import numpy as np
import ml_dtypes


def mxq(x, axis, fmt="e4m3"):
    dtype, down = {"e4m3": (ml_dtypes.float8_e4m3fn, 7), "e5m2": (ml_dtypes.float8_e5m2, 14)}[fmt]
    v = np.moveaxis(np.asarray(x, np.float32).astype(ml_dtypes.bfloat16).astype(np.float64), axis, -1)
    blocks = v.reshape(v.shape[:-1] + (-1, 32))
    amax = np.abs(blocks).max(-1, keepdims=True)
    byte = np.maximum(np.where(amax > 0, np.frexp(amax)[1] - 1 + 127, 0) - down, 1)
    scale = np.exp2(byte - 127.0)
    codes = (blocks / scale).astype(np.float32).astype(dtype).astype(np.float64)
    return np.moveaxis((codes * scale).reshape(v.shape), -1, axis)


WIDE = False


def mx_kscale(k):
    if not WIDE:
        return np.ones(k)
    levels = np.array([10, -10, 5, -5, 0])
    if k % 512:
        return np.exp2(np.random.permutation(np.resize(levels, k // 32))).repeat(32)
    a = np.empty((k // 512, 16))
    for p in range(k // 512):
        a[p, :8] = np.random.permutation(np.resize(levels, 8))
        for g in range(8):
            far = levels[np.abs(levels - a[p, g]) >= 10]
            a[p, g + 8] = far[np.random.randint(len(far))]
    return np.exp2(a.ravel()).repeat(32)


BF16 = ml_dtypes.bfloat16


def bf(x):
    return np.asarray(x, np.float32).astype(BF16)


def f64(x):
    return np.asarray(x).astype(np.float64)


E2M1 = np.array([0.0, 0.5, 1.0, 1.5, 2.0, 3.0, 4.0, 6.0, -0.0, -0.5, -1.0, -1.5, -2.0, -3.0, -4.0, -6.0])


def pack_weight(w, fmt):
    k, n = w.shape
    w = f64(bf(w)).reshape(k // 32, 32, n)
    amax = np.abs(w).max(1)
    if fmt == "e4m3":
        byte = np.frexp(amax)[1] - 1 + 127 - 7
    else:
        mant, ex = np.frexp(amax / 6.0)
        byte = np.where(mant > 0.5, ex, ex - 1) + 127
    byte = np.clip(np.where(amax > 0, byte, 1), 1, 254)
    scaled = (w * np.exp2(127.0 - byte)[:, None, :]).reshape(k, n).astype(np.float32)
    by_word = np.ascontiguousarray(scaled.reshape(k // 512, 128, 4, n).transpose(0, 1, 3, 2))
    if fmt == "e4m3":
        words = by_word.astype(ml_dtypes.float8_e4m3fn).view(np.uint8)
    else:
        c = by_word.astype(ml_dtypes.float4_e2m1fn).view(np.uint8) & 0xF
        words = c[..., 0::2] | (c[..., 1::2] << 4)
    return np.ascontiguousarray(words), np.ascontiguousarray(byte.astype(np.uint8).reshape(k // 512, 16, n))


def unpack_weight(words, scales, fmt):
    g, p, n, _ = words.shape
    if fmt == "e4m3":
        vals = np.ascontiguousarray(words).view(ml_dtypes.float8_e4m3fn).astype(np.float64)
    else:
        nib = np.empty((g, p, n, 4), np.uint8)
        nib[..., 0::2] = words & 0xF
        nib[..., 1::2] = words >> 4
        vals = E2M1[nib]
    vals = vals * np.repeat(np.exp2(scales.astype(np.float64) - 127.0), 8, axis=1)[..., None]
    return vals.transpose(0, 1, 3, 2).reshape(g * 512, n)
def pack4(w):
    words, scales = pack_weight(w, "e2m1")
    return words.reshape(words.shape[0], 128, -1), scales


def unpack4(words, scales):
    return unpack_weight(words.reshape(words.shape[0], 128, -1, 2), scales, "e2m1")


M, J, K, R, V = 1024, 512, 1536, 1024, 2048


def setup_inputs():
    s, u, t = mx_kscale(J), mx_kscale(K), mx_kscale(R)
    x_key = bf(np.random.standard_normal((M, J)) * s)
    x_plant = bf(np.random.standard_normal((M, K)) * u)
    w_key = bf(np.random.standard_normal((J, R)) / np.sqrt(J) / s[:, None])
    plant_words, plant_scales = pack4(np.random.standard_normal((K, R)) / np.sqrt(K) / u[:, None])
    offset = bf(0.3 * np.random.standard_normal(R))
    inv_std = bf(np.random.uniform(0.5, 1.5, R) * t)
    load_words, load_scales = pack4(np.random.standard_normal((R, V)) / np.sqrt(R) / t[:, None])
    return {"x_key": x_key, "x_plant": x_plant, "w_key": w_key,
            "plant_words": plant_words, "plant_scales": plant_scales,
            "offset": offset, "inv_std": inv_std,
            "load_words": load_words, "load_scales": load_scales}


def reference(x_key, x_plant, w_key, plant_words, plant_scales, offset, inv_std, load_words, load_scales):
    w_plant = unpack4(plant_words, plant_scales)
    loadings = unpack4(load_words, load_scales)
    key = mxq(f64(x_key), 1, "e4m3") @ mxq(f64(w_key), 0, "e4m3")
    plant = mxq(f64(x_plant), 1, "e4m3") @ w_plant
    z = (key + plant + f64(offset)) * f64(inv_std)
    d = mxq(z, 1, "e4m3") @ loadings
    contrib = d * d
    stat = contrib.mean(axis=1)
    return contrib, stat

@@ -1,0 +1,272 @@
+from contextlib import ExitStack
+
+import concourse.mybir as mybir
+from concourse.masks import make_identity
+
+F32 = mybir.dt.float32
+BF16 = mybir.dt.bfloat16
+I32 = mybir.dt.int32
+U32 = mybir.dt.uint32
+U8 = mybir.dt.uint8
+FP8X4 = mybir.dt.float8_e4m3fn_x4
+FP4X4 = mybir.dt.float4_e2m1fn_x4
+ACT = mybir.ActivationFunctionType
+ALU = mybir.AluOpType
+
+P = 128
+M, J, K, R, V = 1024, 512, 1536, 1024, 2048
+KEY = 3
+FIRST_G, LAST_G = 0, 3
+VSQ = {(4, 1), (5, 1), (6, 1), (7, 1)}
+ORDER = """
+T:0:0 XO:0:0:S WP:0:0 XQ:0:0
+T:0:1 XO:0:1:S WP:1:0 XQ:0:1
+S1:0:0:0
+T:0:2 XO:0:2:S WP:2:0 XQ:0:2
+S1:0:0:1
+T:0:3 XO:0:3:S WP:0:1 VE:0 KG:0
+S1:0:0:2
+XQ:0:3 KQ:0 WP:1:1
+S1:0:1:0
+S1:0:0:3
+ZO:0:0:S WP:2:1 KG:1
+S1:0:1:1
+S1:0:1:2
+T:1:0 XO:1:0:S KQ:1 XQ:1:0
+T:1:1 XO:1:1:S ZG:0:0 XQ:1:1 ZQ:0:0
+S1:0:1:3
+ZO:0:1:S
+T:1:2 XO:1:2:V XQ:1:2
+S1:1:0:0
+T:1:3 XO:1:3:S ZG:0:1 XQ:1:3 ZQ:0:1
+S1:1:0:1 S1:1:0:2 S1:1:0:3
+ZO:1:0:V S2:0:0 ZG:1:0 ZQ:1:0 S2:0:1 ME:0
+S1:1:1:0 S1:1:1:1 S1:1:1:2 S1:1:1:3
+ME:1 ZO:1:1:V S2:0:2 ZG:1:1 ZQ:1:1 S2:0:3 ME:2
+S2:1:0 ME:3 S2:1:1 ME:4 S2:1:2 ME:5 S2:1:3 ME:6 ME:7
+"""
+FLOPS = 2 * M * R * (J + K) + 2 * M * R * V
+
+
+def tile_hotelling_contribution_monitor_s3_kernel(
+    tc, x_key, x_plant, w_key, plant_words, plant_scales, offset, inv_std, load_words, load_scales_hbm, out_0, out_1
+):
+    nc = tc.nc
+    with ExitStack() as ctx:
+        keep = ctx.enter_context(tc.tile_pool(name="keep", bufs=1))
+        work = ctx.enter_context(tc.tile_pool(name="work", bufs=3))
+        outp = ctx.enter_context(tc.tile_pool(name="outp", bufs=6))
+        psum = ctx.enter_context(tc.psum_pool(name="psum", bufs=8))
+        ctx.enter_context(tc.manual_schedule())
+
+        xk_hbm = x_key.rearrange("(p j) k -> p j k", j=8)
+        xp_hbm = x_plant.rearrange("(p j) k -> p j k", j=8)
+        out_hbm = out_0.rearrange("(p j) v -> p j v", j=8)
+
+        ident = keep.tile([P, P], F32, name="ident")
+        warm = keep.tile([P, 2], F32, name="warm")
+        ps_raw = keep.tile([P, 3 * R], U8, name="ps_raw", align_bytes=64)
+        ls = keep.tile([P, 2 * V], U8, name="ls", align_bytes=64)
+        lw = keep.tile([P, 2, 2 * V], U8, name="lw", align_bytes=64)
+        off_b = keep.tile([P, 8], BF16, name="off_b")
+        inv_b = keep.tile([P, 8], BF16, name="inv_b")
+        vecf = keep.tile([P, 2, 8], F32, name="vecf")
+        zbias = keep.tile([P, 8], F32, name="zbias")
+        acc = keep.tile([P, 8, 4], F32, name="acc")
+        junk = keep.tile([P, 4], F32, name="junk")
+        stat = keep.tile([P, 8], F32, name="stat")
+        x_raw = {}
+        for h in range(2):
+            for g in range(4):
+                x_raw[h, g] = keep.tile([P, 4, 512], BF16, name="x_raw_%d_%d" % (h, g), align_bytes=64)
+        pw_raw = [keep.tile([P, 2048], U8, name="pw_raw_%d" % g, align_bytes=64) for g in range(3)]
+        wk_raw = [keep.tile([P, 4, 512], BF16, name="wk_raw_%d" % s, align_bytes=64) for s in range(2)]
+
+        nc.vector.memset(ps_raw[:].bitcast(I32), 0)
+        nc.vector.memset(warm[:], 0.0)
+        nc.scalar.activation(out=warm[:, 1:2], in_=warm[:, 0:1], func=ACT.Square)
+        make_identity(nc, ident[:])
+        nc.gpsimd.memset(ls[:].bitcast(I32), 0)
+
+        def load_x(h, g):
+            rows = slice(4 * h, 4 * h + 4)
+            src = xk_hbm[:, rows, :] if g == KEY else xp_hbm[:, rows, 512 * g : 512 * g + 512]
+            nc.sync.dma_start(out=x_raw[h, g][:], in_=src)
+
+        wk_hbm = w_key.rearrange("(p j) c -> p j c", j=4)
+        ps_i = ps_raw[:].bitcast(I32).rearrange("p (g n) -> p g n", g=3)
+        ls_i = ls[:].bitcast(I32).rearrange("p (g n) -> p g n", g=2)
+
+        def load_scales(dst, src, queue):
+            for q in range(4):
+                queue.dma_start(
+                    out=dst[32 * q : 32 * q + 4],
+                    in_=src[:, 4 * q : 4 * q + 4, :].bitcast(I32).rearrange("g r n -> r g n"),
+                )
+
+        def load_vector(dst, src):
+            nc.scalar.dma_start(
+                out=dst[:].rearrange("p (s t) -> p s t", s=2), in_=src.rearrange("(s p t) -> p s t", s=2, t=4)
+            )
+
+        for rr in range(2):
+            nc.sync.dma_start(out=x_raw[0, 0][:, 2 * rr : 2 * rr + 2, :], in_=xp_hbm[:, 2 * rr : 2 * rr + 2, 0:512])
+        load_scales(ps_i, plant_scales, nc.scalar)
+        nc.sync.dma_start(out=pw_raw[0][:], in_=plant_words[0])
+        load_x(0, 1)
+        nc.sync.dma_start(out=pw_raw[1][:], in_=plant_words[1])
+        load_x(0, 2)
+        nc.sync.dma_start(out=pw_raw[2][:], in_=plant_words[2])
+        load_x(0, KEY)
+        nc.sync.dma_start(out=wk_raw[0][:], in_=wk_hbm[:, :, 0:512])
+        load_vector(off_b, offset)
+        load_vector(inv_b, inv_std)
+        nc.sync.dma_start(out=wk_raw[1][:], in_=wk_hbm[:, :, 512:1024])
+        for g in range(4):
+            load_x(1, g)
+        load_scales(ls_i, load_scales_hbm, nc.sync)
+        for s in range(2):
+            nc.sync.dma_start(out=lw[:, s, :], in_=load_words[s])
+
+        banks = {}
+        x_grp, x_codes, x_sc = {}, {}, {}
+        p_sc = {}
+        p_codes, k_grp, k_codes, k_sc = {}, {}, {}, {}
+        z_raw, z_grp, z_codes, z_sc = {}, {}, {}, {}
+
+        def transposes(h, g):
+            words = x_raw[h, g][:].bitcast(F32)
+            for b in range(2):
+                bank = psum.tile([P, 512], F32, name="bank")
+                banks["x", h, g, b] = bank
+                for rr in range(2):
+                    for u in range(2):
+                        c = 256 * rr + 128 * u
+                        nc.tensor.transpose(bank[:, c : c + 128], words[:, 2 * b + rr, u::2], ident[:])
+
+        def x_out(h, g, engine):
+            x_grp[h, g] = work.tile([P, 2048], BF16, name="x_grp", align_bytes=64)
+            words = x_grp[h, g][:].bitcast(F32)
+            for b in range(2):
+                src = banks["x", h, g, b][:].rearrange("p (r u n) -> p r n u", r=2, u=2)
+                dst = words[:, 512 * b : 512 * b + 512].rearrange("p (r n u) -> p r n u", r=2, u=2)
+                if engine == "S" or (engine == "SV" and b == 0):
+                    nc.scalar.copy(out=dst, in_=src)
+                else:
+                    nc.vector.tensor_copy(out=dst, in_=src)
+
+        def x_quant(h, g):
+            x_codes[h, g] = keep.tile([P, 512], U32, name="x_codes_%d_%d" % (h, g), align_bytes=64)
+            x_sc[h, g] = keep.tile([P, 512], U8, name="x_sc_%d_%d" % (h, g), align_bytes=64)
+            nc.vector.quantize_mx(out=x_codes[h, g][:].bitcast(FP8X4), scales=x_sc[h, g][:], in_=x_grp[h, g][:])
+
+        def words_perm(g, s):
+            p_codes[g, s] = keep.tile([P, 1024], U8, name="p_codes_%d_%d" % (g, s), align_bytes=64)
+            p_sc[g, s] = keep.tile([P, 512], U8, name="p_sc_%d_%d" % (g, s), align_bytes=64)
+            nc.vector.tensor_copy(
+                out=p_codes[g, s][:].rearrange("p (t m b) -> p t m b", t=4, b=2),
+                in_=pw_raw[g][:, 1024 * s : 1024 * s + 1024].rearrange("p (m t b) -> p t m b", t=4, b=2),
+            )
+            nc.vector.tensor_copy(
+                out=p_sc[g, s][:].rearrange("p (t m) -> p t m", t=4),
+                in_=ps_raw[:, R * g + 512 * s : R * g + 512 * s + 512].rearrange("p (m t) -> p t m", t=4),
+            )
+
+        def key_group(s):
+            k_grp[s] = work.tile([P, 2048], BF16, name="k_grp", align_bytes=64)
+            nc.vector.tensor_copy(
+                out=k_grp[s][:].rearrange("p (t m j) -> p t m j", t=4, j=4),
+                in_=wk_raw[s][:].rearrange("p j (m t) -> p t m j", t=4),
+            )
+
+        def key_quant(s):
+            k_codes[s] = keep.tile([P, 512], U32, name="k_codes_%d" % s, align_bytes=64)
+            k_sc[s] = keep.tile([P, 512], U8, name="k_sc_%d" % s, align_bytes=64)
+            nc.vector.quantize_mx(out=k_codes[s][:].bitcast(FP8X4), scales=k_sc[s][:], in_=k_grp[s][:])
+
+        def stage1(h, s, g):
+            first, last = g == FIRST_G, g == LAST_G
+            for t in range(4):
+                if first:
+                    bank = psum.tile([P, 512], F32, name="bank")
+                    banks["s", h, s, t] = bank
+                cols = slice(128 * t, 128 * t + 128)
+                if g == KEY:
+                    lhs, lhs_sc = k_codes[s][:, cols].bitcast(FP8X4), k_sc[s][:, cols]
+                else:
+                    lhs = p_codes[g, s][:, 256 * t : 256 * t + 256].bitcast(FP4X4)
+                    lhs_sc = p_sc[g, s][:, cols]
+                nc.tensor.matmul_mx(
+                    out=banks["s", h, s, t][:], lhsT=lhs, lhsT_scale=lhs_sc,
+                    rhs=x_codes[h, g][:].bitcast(FP8X4), rhs_scale=x_sc[h, g][:], start=first, stop=last,
+                )
+
+        def z_out(h, s, engine):
+            z_raw[h, s] = work.tile([P, 4, 512], BF16, name="z_raw", align_bytes=64)
+            for t in range(4):
+                c = 4 * s + t
+                if engine == "S":
+                    nc.scalar.activation(
+                        out=z_raw[h, s][:, t, :], in_=banks["s", h, s, t][:], func=ACT.Identity,
+                        bias=zbias[:, c : c + 1], scale=vecf[:, 1, c : c + 1],
+                    )
+                else:
+                    nc.vector.tensor_scalar(
+                        out=z_raw[h, s][:, t, :], in0=banks["s", h, s, t][:], scalar1=vecf[:, 0, c : c + 1],
+                        scalar2=vecf[:, 1, c : c + 1], op0=ALU.add, op1=ALU.mult,
+                    )
+
+        def z_group(h, s):
+            z_grp[h, s] = work.tile([P, 2048], BF16, name="z_grp", align_bytes=64)
+            nc.vector.tensor_copy(
+                out=z_grp[h, s][:].rearrange("p (n t) -> p n t", t=4), in_=z_raw[h, s][:].rearrange("p t n -> p n t")
+            )
+
+        def z_quant(h, s):
+            z_codes[h, s] = keep.tile([P, 512], U32, name="z_codes_%d_%d" % (h, s), align_bytes=64)
+            z_sc[h, s] = keep.tile([P, 512], U8, name="z_sc_%d_%d" % (h, s), align_bytes=64)
+            nc.vector.quantize_mx(out=z_codes[h, s][:].bitcast(FP8X4), scales=z_sc[h, s][:], in_=z_grp[h, s][:])
+
+        def stage2(h, r):
+            j = 4 * h + r
+            cols = slice(128 * r, 128 * r + 128)
+            for w in range(2):
+                res = outp.tile([P, 1024], F32, name="res")
+                for vv in range(2):
+                    v = 2 * w + vv
+                    bank = psum.tile([P, 512], F32, name="bank")
+                    for s in range(2):
+                        nc.tensor.matmul_mx(
+                            out=bank[:], lhsT=z_codes[h, s][:, cols].bitcast(FP8X4), lhsT_scale=z_sc[h, s][:, cols],
+                            rhs=lw[:, s, 1024 * v : 1024 * v + 1024].bitcast(FP4X4),
+                            rhs_scale=ls[:, V * s + 512 * v : V * s + 512 * v + 512], start=s == 0, stop=s == 1,
+                        )
+                    half = res[:, 512 * vv : 512 * vv + 512]
+                    if (j, v) in VSQ:
+                        copy = work.tile([P, 512], F32, name="copy")
+                        nc.vector.tensor_copy(out=copy[:], in_=bank[:])
+                        nc.vector.scalar_tensor_tensor(
+                            out=half, in0=bank[:], scalar=1.0, in1=copy[:], op0=ALU.mult, op1=ALU.mult,
+                            accum_out=acc[:, j, v : v + 1],
+                        )
+                    else:
+                        nc.scalar.activation(out=half, in_=bank[:], func=ACT.Square, accum_out=acc[:, j, v : v + 1])
+                nc.sync.dma_start(out=out_hbm[:, j, 1024 * w : 1024 * w + 1024], in_=res[:])
+
+        def mean(j):
+            nc.scalar.activation(out=junk[:], in_=acc[:, j, :], func=ACT.Copy, scale=1.0 / V, accum_out=stat[:, j : j + 1])
+
+        def vectors(unused):
+            nc.vector.tensor_copy(out=vecf[:, 0, :], in_=off_b[:])
+            nc.vector.tensor_copy(out=vecf[:, 1, :], in_=inv_b[:])
+            nc.vector.tensor_tensor(out=zbias[:], in0=vecf[:, 0, :], in1=vecf[:, 1, :], op=ALU.mult)
+
+        calls = {
+            "T": transposes, "XO": x_out, "XQ": x_quant, "WP": words_perm, "KG": key_group,
+            "KQ": key_quant, "S1": stage1, "ZO": z_out, "ZG": z_group, "ZQ": z_quant, "S2": stage2, "ME": mean, "VE": vectors,
+        }
+        for step in ORDER.split():
+            parts = step.split(":")
+            args = [a if a in ("S", "V", "SV") else int(a) for a in parts[1:]]
+            calls[parts[0]](*args)
+        nc.sync.dma_start(out=out_1.rearrange("(p j) -> p j", j=8), in_=stat[:])

@@ -17,32 +17,38 @@ P = 128
 M, J, K, R, V = 1024, 512, 1536, 1024, 2048
 KEY = 3
 FIRST_G, LAST_G = 0, 3
-VSQ = {(4, 1), (5, 1), (6, 1), (7, 1)}
+VSQ = {(2, 1), (3, 1), (4, 1), (5, 1), (6, 1), (7, 1)}
 ORDER = """
-T:0:0 XO:0:0:S WP:0:0 XQ:0:0
-T:0:1 XO:0:1:S WP:1:0 XQ:0:1
+W:6 WW:0:0
+T:0:0 XO:0:0:S WW:1:0 WS:0:0 XQ:0:0 W:3
+T:0:1 XO:0:1:S WS:1:0 XQ:0:1
+T:0:2 XO:0:2:S
 S1:0:0:0
-T:0:2 XO:0:2:S WP:2:0 XQ:0:2
+KG:0:S
+T:0:3 XO:0:3:S WW:2:0 WS:2:0 XQ:0:2
 S1:0:0:1
-T:0:3 XO:0:3:S WP:0:1 VE:0 KG:0
+VE:0 WS:0:1 KQ:0 XQ:0:3
 S1:0:0:2
-XQ:0:3 KQ:0 WP:1:1
-S1:0:1:0
-S1:0:0:3
-ZO:0:0:S WP:2:1 KG:1
-S1:0:1:1
-S1:0:1:2
-T:1:0 XO:1:0:S KQ:1 XQ:1:0
-T:1:1 XO:1:1:S ZG:0:0 XQ:1:1 ZQ:0:0
-S1:0:1:3
-ZO:0:1:S
-T:1:2 XO:1:2:V XQ:1:2
-S1:1:0:0
-T:1:3 XO:1:3:S ZG:0:1 XQ:1:3 ZQ:0:1
-S1:1:0:1 S1:1:0:2 S1:1:0:3
-ZO:1:0:V S2:0:0 ZG:1:0 ZQ:1:0 S2:0:1 ME:0
-S1:1:1:0 S1:1:1:1 S1:1:1:2 S1:1:1:3
-ME:1 ZO:1:1:V S2:0:2 ZG:1:1 ZQ:1:1 S2:0:3 ME:2
+WS:1:1 
+XP:1:2:S XP:1:3:S
+T:1:0 XO:1:0:S WS:2:1 T:1:1 XO:1:1:S
+S1:0:0:3 ZO:0:0:S
+WW:0:1 XQ:1:0 WW:1:1 XQ:1:1
+T:1:2 T:1:3 XO:1:2:S XO:1:3:S
+S1:0:1:0 WW:2:1 KG:1:V KQ:1
+S1:0:1:1 XQ:1:2 
+S1:0:1:2 XQ:1:3 ZG:0:0
+S1:0:1:3 ZQ:0:0 ZO:0:1:S
+S1:1:0:0 S1:1:0:1
+S1:1:0:2 ZG:0:1
+S1:1:0:3 ZQ:0:1 ZO:1:0:S
+S1:1:1:0 S1:1:1:1 ZG:1:0
+S1:1:1:2 ZQ:1:0
+S1:1:1:3 
+S2:0:0 ZO:1:1:V
+S2:0:1 ME:0 ZG:1:1
+S2:0:2 ME:1 ZQ:1:1
+S2:0:3 ME:2
 S2:1:0 ME:3 S2:1:1 ME:4 S2:1:2 ME:5 S2:1:3 ME:6 ME:7
 """
 FLOPS = 2 * M * R * (J + K) + 2 * M * R * V
@@ -79,9 +85,11 @@ def tile_hotelling_contribution_monitor_s3_kernel(
         for h in range(2):
             for g in range(4):
                 x_raw[h, g] = keep.tile([P, 4, 512], BF16, name="x_raw_%d_%d" % (h, g), align_bytes=64)
-        pw_raw = [keep.tile([P, 2048], U8, name="pw_raw_%d" % g, align_bytes=64) for g in range(3)]
+        pw_raw = keep.tile([P, 2, 3, 1024], U8, name="pw_raw", align_bytes=64)
         wk_raw = [keep.tile([P, 4, 512], BF16, name="wk_raw_%d" % s, align_bytes=64) for s in range(2)]
 
+        dummy = keep.tile([P, 512], BF16, name="dummy")
+        nc.vector.memset(dummy[:], 0.0)
         nc.vector.memset(ps_raw[:].bitcast(I32), 0)
         nc.vector.memset(warm[:], 0.0)
         nc.scalar.activation(out=warm[:, 1:2], in_=warm[:, 0:1], func=ACT.Square)
@@ -109,26 +117,31 @@ def tile_hotelling_contribution_monitor_s3_kernel(
                 out=dst[:].rearrange("p (s t) -> p s t", s=2), in_=src.rearrange("(s p t) -> p s t", s=2, t=4)
             )
 
+        def load_words_plant(s, g0, g1):
+            src = plant_words.rearrange("g p (s b) -> s p g b", s=2)
+            nc.sync.dma_start(out=pw_raw[:, s, g0:g1, :], in_=src[s, :, g0:g1, :])
+
+        load_words_plant(0, 0, 1)
+        load_scales(ps_i, plant_scales, nc.scalar)
         for rr in range(2):
             nc.sync.dma_start(out=x_raw[0, 0][:, 2 * rr : 2 * rr + 2, :], in_=xp_hbm[:, 2 * rr : 2 * rr + 2, 0:512])
-        load_scales(ps_i, plant_scales, nc.scalar)
-        nc.sync.dma_start(out=pw_raw[0][:], in_=plant_words[0])
         load_x(0, 1)
-        nc.sync.dma_start(out=pw_raw[1][:], in_=plant_words[1])
+        load_words_plant(0, 1, 3)
         load_x(0, 2)
-        nc.sync.dma_start(out=pw_raw[2][:], in_=plant_words[2])
         load_x(0, KEY)
         nc.sync.dma_start(out=wk_raw[0][:], in_=wk_hbm[:, :, 0:512])
         load_vector(off_b, offset)
         load_vector(inv_b, inv_std)
-        nc.sync.dma_start(out=wk_raw[1][:], in_=wk_hbm[:, :, 512:1024])
         for g in range(4):
             load_x(1, g)
+        load_words_plant(1, 0, 3)
+        nc.sync.dma_start(out=wk_raw[1][:], in_=wk_hbm[:, :, 512:1024])
         load_scales(ls_i, load_scales_hbm, nc.sync)
         for s in range(2):
             nc.sync.dma_start(out=lw[:, s, :], in_=load_words[s])
 
         banks = {}
+        x_perm = {}
         x_grp, x_codes, x_sc = {}, {}, {}
         p_sc = {}
         p_codes, k_grp, k_codes, k_sc = {}, {}, {}, {}
@@ -137,12 +150,25 @@ def tile_hotelling_contribution_monitor_s3_kernel(
         def transposes(h, g):
             words = x_raw[h, g][:].bitcast(F32)
             for b in range(2):
+                if (h, g) in x_perm:
+                    perm = x_perm[h, g]
                 bank = psum.tile([P, 512], F32, name="bank")
                 banks["x", h, g, b] = bank
                 for rr in range(2):
                     for u in range(2):
                         c = 256 * rr + 128 * u
-                        nc.tensor.transpose(bank[:, c : c + 128], words[:, 2 * b + rr, u::2], ident[:])
+                        if (h, g) in x_perm:
+                            nc.tensor.transpose(bank[:, c : c + 128], perm[:, 2 * b + rr, u, :], ident[:])
+                        else:
+                            nc.tensor.transpose(bank[:, c : c + 128], words[:, 2 * b + rr, u::2], ident[:])
+
+        def x_order(h, g, engine):
+            x_perm[h, g] = work.tile([P, 4, 2, 128], F32, name="x_perm", align_bytes=64)
+            src = x_raw[h, g][:].bitcast(F32).rearrange("p r (n u) -> p r u n", u=2)
+            if engine == "S":
+                nc.scalar.copy(out=x_perm[h, g][:], in_=src)
+            else:
+                nc.vector.tensor_copy(out=x_perm[h, g][:], in_=src)
 
         def x_out(h, g, engine):
             x_grp[h, g] = work.tile([P, 2048], BF16, name="x_grp", align_bytes=64)
@@ -162,22 +188,29 @@ def tile_hotelling_contribution_monitor_s3_kernel(
 
         def words_perm(g, s):
             p_codes[g, s] = keep.tile([P, 1024], U8, name="p_codes_%d_%d" % (g, s), align_bytes=64)
-            p_sc[g, s] = keep.tile([P, 512], U8, name="p_sc_%d_%d" % (g, s), align_bytes=64)
             nc.vector.tensor_copy(
                 out=p_codes[g, s][:].rearrange("p (t m b) -> p t m b", t=4, b=2),
-                in_=pw_raw[g][:, 1024 * s : 1024 * s + 1024].rearrange("p (m t b) -> p t m b", t=4, b=2),
+                in_=pw_raw[:, s, g, :].rearrange("p (m t b) -> p t m b", t=4, b=2),
             )
+
+        def scales_perm(g, s):
+            p_sc[g, s] = keep.tile([P, 512], U8, name="p_sc_%d_%d" % (g, s), align_bytes=64)
             nc.vector.tensor_copy(
                 out=p_sc[g, s][:].rearrange("p (t m) -> p t m", t=4),
                 in_=ps_raw[:, R * g + 512 * s : R * g + 512 * s + 512].rearrange("p (m t) -> p t m", t=4),
             )
 
-        def key_group(s):
+        def key_group(s, engine):
             k_grp[s] = work.tile([P, 2048], BF16, name="k_grp", align_bytes=64)
-            nc.vector.tensor_copy(
-                out=k_grp[s][:].rearrange("p (t m j) -> p t m j", t=4, j=4),
-                in_=wk_raw[s][:].rearrange("p j (m t) -> p t m j", t=4),
-            )
+            dst = k_grp[s][:].rearrange("p (t m j) -> p t m j", t=4, j=4)
+            src = wk_raw[s][:].rearrange("p j (m t) -> p t m j", t=4)
+            if engine == "S":
+                nc.scalar.copy(out=dst, in_=src)
+            elif engine == "V":
+                nc.vector.tensor_copy(out=dst, in_=src)
+            else:
+                nc.scalar.copy(out=dst[:, 0:2], in_=src[:, 0:2])
+                nc.vector.tensor_copy(out=dst[:, 2:4], in_=src[:, 2:4])
 
         def key_quant(s):
             k_codes[s] = keep.tile([P, 512], U32, name="k_codes_%d" % s, align_bytes=64)
@@ -205,7 +238,7 @@ def tile_hotelling_contribution_monitor_s3_kernel(
             z_raw[h, s] = work.tile([P, 4, 512], BF16, name="z_raw", align_bytes=64)
             for t in range(4):
                 c = 4 * s + t
-                if engine == "S":
+                if engine == "S" or (engine == "SV" and t < 2):
                     nc.scalar.activation(
                         out=z_raw[h, s][:, t, :], in_=banks["s", h, s, t][:], func=ACT.Identity,
                         bias=zbias[:, c : c + 1], scale=vecf[:, 1, c : c + 1],
@@ -251,10 +284,18 @@ def tile_hotelling_contribution_monitor_s3_kernel(
                         )
                     else:
                         nc.scalar.activation(out=half, in_=bank[:], func=ACT.Square, accum_out=acc[:, j, v : v + 1])
-                nc.sync.dma_start(out=out_hbm[:, j, 1024 * w : 1024 * w + 1024], in_=res[:])
+                    if j == 7:
+                        nc.sync.dma_start(out=out_hbm[:, j, 512 * v : 512 * v + 512], in_=half)
+                if j != 7:
+                    nc.sync.dma_start(out=out_hbm[:, j, 1024 * w : 1024 * w + 1024], in_=res[:])
 
         def mean(j):
             nc.scalar.activation(out=junk[:], in_=acc[:, j, :], func=ACT.Copy, scale=1.0 / V, accum_out=stat[:, j : j + 1])
+
+        def warm_up(n):
+            bank = psum.tile([P, 512], F32, name="bank")
+            for i in range(n):
+                nc.tensor.matmul(bank[:], lhsT=dummy[:, 0:128], rhs=dummy[:], start=True, stop=True)
 
         def vectors(unused):
             nc.vector.tensor_copy(out=vecf[:, 0, :], in_=off_b[:])
@@ -262,8 +303,8 @@ def tile_hotelling_contribution_monitor_s3_kernel(
             nc.vector.tensor_tensor(out=zbias[:], in0=vecf[:, 0, :], in1=vecf[:, 1, :], op=ALU.mult)
 
         calls = {
-            "T": transposes, "XO": x_out, "XQ": x_quant, "WP": words_perm, "KG": key_group,
-            "KQ": key_quant, "S1": stage1, "ZO": z_out, "ZG": z_group, "ZQ": z_quant, "S2": stage2, "ME": mean, "VE": vectors,
+            "T": transposes, "XO": x_out, "XQ": x_quant, "WW": words_perm, "WS": scales_perm, "KG": key_group,
+            "KQ": key_quant, "S1": stage1, "ZO": z_out, "ZG": z_group, "ZQ": z_quant, "S2": stage2, "ME": mean, "VE": vectors, "W": warm_up, "XP": x_order,
         }
         for step in ORDER.split():
             parts = step.split(":")

@@ -19,33 +19,30 @@ KEY = 3
 FIRST_G, LAST_G = 0, 3
 VSQ = {(2, 1), (3, 1), (4, 1), (5, 1), (6, 1), (7, 1)}
 ORDER = """
-W:6 WW:0:0
-T:0:0 XO:0:0:S WW:1:0 WS:0:0 XQ:0:0 W:3
-T:0:1 XO:0:1:S WS:1:0 XQ:0:1
-T:0:2 XO:0:2:S
+LP:0:0:1 LS:0 LF:0 LF:1 LX:0:1 LX:0:3 LX:0:2 LP:0:1:3 LV:0 LX:1:0 LX:1:1 LP:1:0:3 LK:0 LX:1:2 LX:1:3 LK:1 LL:0
+
+W:5 WW:0:0
+T:0:0 XO:0:0:S WS:0:0 XQ:0:0 W:3
+T:0:1 XO:0:1:S T:0:3 WS:0:1 WS:2:1
 S1:0:0:0
-KG:0:S
-T:0:3 XO:0:3:S WW:2:0 WS:2:0 XQ:0:2
+T:0:2 XQ:0:1 XO:0:3:S WS:1:0 WW:1:0 XO:0:2:S
 S1:0:0:1
-VE:0 WS:0:1 KQ:0 XQ:0:3
+WW:2:0 XP:1:1:S WS:1:1 WS:2:0 XQ:0:2
+T:1:0 T:1:1 XO:1:0:S XO:1:1:S WW:0:1
 S1:0:0:2
-WS:1:1 
-XP:1:2:S XP:1:3:S
-T:1:0 XO:1:0:S WS:2:1 T:1:1 XO:1:1:S
-S1:0:0:3 ZO:0:0:S
-WW:0:1 XQ:1:0 WW:1:1 XQ:1:1
-T:1:2 T:1:3 XO:1:2:S XO:1:3:S
-S1:0:1:0 WW:2:1 KG:1:V KQ:1
-S1:0:1:1 XQ:1:2 
-S1:0:1:2 XQ:1:3 ZG:0:0
-S1:0:1:3 ZQ:0:0 ZO:0:1:S
-S1:1:0:0 S1:1:0:1
-S1:1:0:2 ZG:0:1
-S1:1:0:3 ZQ:0:1 ZO:1:0:S
-S1:1:1:0 S1:1:1:1 ZG:1:0
-S1:1:1:2 ZQ:1:0
-S1:1:1:3 
-S2:0:0 ZO:1:1:V
+WW:1:1 XQ:0:3 VE:0 KG:0:S XP:1:2:S
+S1:0:1:0
+KQ:0 WW:2:1
+S1:0:1:1 S1:0:0:3
+KG:1:V XP:1:3:S KQ:1
+S1:0:1:2 ZO:0:0:S
+T:1:2 T:1:3 XO:1:2:S XO:1:3:S XQ:1:0 XQ:1:1
+S1:0:1:3 ZO:0:1:S
+XQ:1:2 ZG:0:0 XQ:1:3
+S1:1:0:0 S1:1:0:1 ZQ:0:0 ZG:0:1
+S1:1:0:2 S1:1:0:3 ZO:1:0:S ZQ:0:1
+S1:1:1:0 S1:1:1:1 S1:1:1:2 S1:1:1:3 ZG:1:0 ZO:1:1:V
+S2:0:0 ZQ:1:0
 S2:0:1 ME:0 ZG:1:1
 S2:0:2 ME:1 ZQ:1:1
 S2:0:3 ME:2
@@ -60,7 +57,7 @@ def tile_hotelling_contribution_monitor_s3_kernel(
     nc = tc.nc
     with ExitStack() as ctx:
         keep = ctx.enter_context(tc.tile_pool(name="keep", bufs=1))
-        work = ctx.enter_context(tc.tile_pool(name="work", bufs=3))
+        work = ctx.enter_context(tc.tile_pool(name="work", bufs=4))
         outp = ctx.enter_context(tc.tile_pool(name="outp", bufs=6))
         psum = ctx.enter_context(tc.psum_pool(name="psum", bufs=8))
         ctx.enter_context(tc.manual_schedule())
@@ -78,8 +75,8 @@ def tile_hotelling_contribution_monitor_s3_kernel(
         inv_b = keep.tile([P, 8], BF16, name="inv_b")
         vecf = keep.tile([P, 2, 8], F32, name="vecf")
         zbias = keep.tile([P, 8], F32, name="zbias")
-        acc = keep.tile([P, 8, 4], F32, name="acc")
-        junk = keep.tile([P, 4], F32, name="junk")
+        acc = keep.tile([P, 8, 5], F32, name="acc")
+        junk = keep.tile([P, 5], F32, name="junk")
         stat = keep.tile([P, 8], F32, name="stat")
         x_raw = {}
         for h in range(2):
@@ -89,8 +86,8 @@ def tile_hotelling_contribution_monitor_s3_kernel(
         wk_raw = [keep.tile([P, 4, 512], BF16, name="wk_raw_%d" % s, align_bytes=64) for s in range(2)]
 
         dummy = keep.tile([P, 512], BF16, name="dummy")
-        nc.vector.memset(dummy[:], 0.0)
         nc.vector.memset(ps_raw[:].bitcast(I32), 0)
+        nc.vector.memset(dummy[:], 0.0)
         nc.vector.memset(warm[:], 0.0)
         nc.scalar.activation(out=warm[:, 1:2], in_=warm[:, 0:1], func=ACT.Square)
         make_identity(nc, ident[:])
@@ -113,7 +110,7 @@ def tile_hotelling_contribution_monitor_s3_kernel(
                 )
 
         def load_vector(dst, src):
-            nc.scalar.dma_start(
+            nc.sync.dma_start(
                 out=dst[:].rearrange("p (s t) -> p s t", s=2), in_=src.rearrange("(s p t) -> p s t", s=2, t=4)
             )
 
@@ -121,24 +118,23 @@ def tile_hotelling_contribution_monitor_s3_kernel(
             src = plant_words.rearrange("g p (s b) -> s p g b", s=2)
             nc.sync.dma_start(out=pw_raw[:, s, g0:g1, :], in_=src[s, :, g0:g1, :])
 
-        load_words_plant(0, 0, 1)
-        load_scales(ps_i, plant_scales, nc.scalar)
-        for rr in range(2):
+        def load_first(rr):
             nc.sync.dma_start(out=x_raw[0, 0][:, 2 * rr : 2 * rr + 2, :], in_=xp_hbm[:, 2 * rr : 2 * rr + 2, 0:512])
-        load_x(0, 1)
-        load_words_plant(0, 1, 3)
-        load_x(0, 2)
-        load_x(0, KEY)
-        nc.sync.dma_start(out=wk_raw[0][:], in_=wk_hbm[:, :, 0:512])
-        load_vector(off_b, offset)
-        load_vector(inv_b, inv_std)
-        for g in range(4):
-            load_x(1, g)
-        load_words_plant(1, 0, 3)
-        nc.sync.dma_start(out=wk_raw[1][:], in_=wk_hbm[:, :, 512:1024])
-        load_scales(ls_i, load_scales_hbm, nc.sync)
-        for s in range(2):
-            nc.sync.dma_start(out=lw[:, s, :], in_=load_words[s])
+
+        def load_key(s):
+            nc.sync.dma_start(out=wk_raw[s][:], in_=wk_hbm[:, :, 512 * s : 512 * s + 512])
+
+        def load_vectors(unused):
+            load_vector(off_b, offset)
+            load_vector(inv_b, inv_std)
+
+        def load_plant_scales(unused):
+            load_scales(ps_i, plant_scales, nc.scalar)
+
+        def load_load(unused):
+            load_scales(ls_i, load_scales_hbm, nc.sync)
+            for s in range(2):
+                nc.sync.dma_start(out=lw[:, s, :], in_=load_words[s])
 
         banks = {}
         x_perm = {}
@@ -252,7 +248,8 @@ def tile_hotelling_contribution_monitor_s3_kernel(
         def z_group(h, s):
             z_grp[h, s] = work.tile([P, 2048], BF16, name="z_grp", align_bytes=64)
             nc.vector.tensor_copy(
-                out=z_grp[h, s][:].rearrange("p (n t) -> p n t", t=4), in_=z_raw[h, s][:].rearrange("p t n -> p n t")
+                out=z_grp[h, s][:].rearrange("p (n i t) -> p n t i", t=4, i=4),
+                in_=z_raw[h, s][:].rearrange("p t (n i) -> p n t i", i=4),
             )
 
         def z_quant(h, s):
@@ -275,6 +272,16 @@ def tile_hotelling_contribution_monitor_s3_kernel(
                             rhs_scale=ls[:, V * s + 512 * v : V * s + 512 * v + 512], start=s == 0, stop=s == 1,
                         )
                     half = res[:, 512 * vv : 512 * vv + 512]
+                    if (j, v) == (7, 3):
+                        for c in (0, 256):
+                            nc.scalar.activation(
+                                out=half[:, c : c + 256], in_=bank[:, c : c + 256], func=ACT.Square,
+                                accum_out=acc[:, j, 3 + c // 256 : 4 + c // 256],
+                            )
+                            nc.sync.dma_start(
+                                out=out_hbm[:, j, 512 * v + c : 512 * v + c + 256], in_=half[:, c : c + 256]
+                            )
+                        continue
                     if (j, v) in VSQ:
                         copy = work.tile([P, 512], F32, name="copy")
                         nc.vector.tensor_copy(out=copy[:], in_=bank[:])
@@ -290,7 +297,8 @@ def tile_hotelling_contribution_monitor_s3_kernel(
                     nc.sync.dma_start(out=out_hbm[:, j, 1024 * w : 1024 * w + 1024], in_=res[:])
 
         def mean(j):
-            nc.scalar.activation(out=junk[:], in_=acc[:, j, :], func=ACT.Copy, scale=1.0 / V, accum_out=stat[:, j : j + 1])
+            n = 5 if j == 7 else 4
+            nc.scalar.activation(out=junk[:, 0:n], in_=acc[:, j, 0:n], func=ACT.Copy, scale=1.0 / V, accum_out=stat[:, j : j + 1])
 
         def warm_up(n):
             bank = psum.tile([P, 512], F32, name="bank")
@@ -304,7 +312,8 @@ def tile_hotelling_contribution_monitor_s3_kernel(
 
         calls = {
             "T": transposes, "XO": x_out, "XQ": x_quant, "WW": words_perm, "WS": scales_perm, "KG": key_group,
-            "KQ": key_quant, "S1": stage1, "ZO": z_out, "ZG": z_group, "ZQ": z_quant, "S2": stage2, "ME": mean, "VE": vectors, "W": warm_up, "XP": x_order,
+            "KQ": key_quant, "S1": stage1, "ZO": z_out, "ZG": z_group, "ZQ": z_quant, "S2": stage2, "ME": mean, "VE": vectors, "W": warm_up, "LX": load_x, "LF": load_first, "LP": load_words_plant, "LK": load_key, "LV": load_vectors,
+            "LS": load_plant_scales, "LL": load_load, "XP": x_order,
         }
         for step in ORDER.split():
             parts = step.split(":")

@@ -17,31 +17,30 @@ P = 128
 M, J, K, R, V = 1024, 512, 1536, 1024, 2048
 KEY = 3
 FIRST_G, LAST_G = 0, 3
-VSQ = {(2, 1), (3, 1), (4, 1), (5, 1), (6, 1), (7, 1)}
+VSQ = {(3, 1), (4, 1), (5, 1), (6, 1), (7, 1)}
 ORDER = """
-LP:0:0:1 LS:0 LF:0 LF:1 LX:0:1 LX:0:3 LX:0:2 LP:0:1:3 LV:0 LX:1:0 LX:1:1 LP:1:0:3 LK:0 LX:1:2 LX:1:3 LK:1 LL:0
+LP:0:0:1 LS:0 LF:0 LF:1 LX:0:1 LX:0:3 LX:1:0 LP:0:1:3 LX:0:2 LP:1:0:3 LK:0 LX:1:1 LX:1:2 LV:0 LX:1:3 LK:1 LL:0
 
-W:5 WW:0:0
-T:0:0 XO:0:0:S WS:0:0 XQ:0:0 W:3
-T:0:1 XO:0:1:S T:0:3 WS:0:1 WS:2:1
+W:8 WW:0:0
+T:0:0 XO:0:0:S WS:0:0
+T:0:1 XO:0:1:S WS:1:0 XQ:0:0 WS:2:0 WS:0:1 XQ:0:1
+T:0:3 XO:0:3:S WW:1:0 XP:1:0:S
 S1:0:0:0
-T:0:2 XQ:0:1 XO:0:3:S WS:1:0 WW:1:0 XO:0:2:S
+T:0:2 XO:0:2:S WW:2:0
 S1:0:0:1
-WW:2:0 XP:1:1:S WS:1:1 WS:2:0 XQ:0:2
-T:1:0 T:1:1 XO:1:0:S XO:1:1:S WW:0:1
+WW:0:1 T:1:0 XO:1:0:S KG:0:V XQ:0:2 KQ:0
+T:1:1 XO:1:1:S XQ:0:3 VE:0 WW:1:1 WS:1:1 WS:2:1
 S1:0:0:2
-WW:1:1 XQ:0:3 VE:0 KG:0:S XP:1:2:S
-S1:0:1:0
-KQ:0 WW:2:1
-S1:0:1:1 S1:0:0:3
-KG:1:V XP:1:3:S KQ:1
-S1:0:1:2 ZO:0:0:S
-T:1:2 T:1:3 XO:1:2:S XO:1:3:S XQ:1:0 XQ:1:1
+WW:2:1
+S1:0:0:3 XP:1:2:S ZO:0:0:S KG:1:V
+S1:0:1:0 S1:0:1:1 
+S1:0:1:2 KQ:1 XQ:1:0 XP:1:3:S
+T:1:2 T:1:3 XO:1:2:S XQ:1:1 XQ:1:2 XO:1:3:S
 S1:0:1:3 ZO:0:1:S
-XQ:1:2 ZG:0:0 XQ:1:3
-S1:1:0:0 S1:1:0:1 ZQ:0:0 ZG:0:1
-S1:1:0:2 S1:1:0:3 ZO:1:0:S ZQ:0:1
-S1:1:1:0 S1:1:1:1 S1:1:1:2 S1:1:1:3 ZG:1:0 ZO:1:1:V
+XQ:1:3 S1:1:0:0 ZG:0:0
+S1:1:0:1 ZQ:0:0
+S1:1:0:2 S1:1:0:3 ZG:0:1 ZO:1:0:S
+S1:1:1:0 S1:1:1:1 ZQ:0:1 S1:1:1:2 S1:1:1:3 ZG:1:0 ZO:1:1:V
 S2:0:0 ZQ:1:0
 S2:0:1 ME:0 ZG:1:1
 S2:0:2 ME:1 ZQ:1:1
@@ -248,8 +247,7 @@ def tile_hotelling_contribution_monitor_s3_kernel(
         def z_group(h, s):
             z_grp[h, s] = work.tile([P, 2048], BF16, name="z_grp", align_bytes=64)
             nc.vector.tensor_copy(
-                out=z_grp[h, s][:].rearrange("p (n i t) -> p n t i", t=4, i=4),
-                in_=z_raw[h, s][:].rearrange("p t (n i) -> p n t i", i=4),
+                out=z_grp[h, s][:].rearrange("p (n t) -> p n t", t=4), in_=z_raw[h, s][:].rearrange("p t n -> p n t")
             )
 
         def z_quant(h, s):

@@ -17,35 +17,31 @@ P = 128
 M, J, K, R, V = 1024, 512, 1536, 1024, 2048
 KEY = 3
 FIRST_G, LAST_G = 0, 3
-VSQ = {(3, 1), (4, 1), (5, 1), (6, 1), (7, 1)}
+VSQ = {(2, 1), (3, 1), (4, 1), (5, 1), (6, 1), (7, 1)}
 ORDER = """
-LP:0:0:1 LS:0 LF:0 LF:1 LX:0:1 LX:0:3 LX:1:0 LP:0:1:3 LX:0:2 LP:1:0:3 LK:0 LX:1:1 LX:1:2 LV:0 LX:1:3 LK:1 LL:0
-
-W:8 WW:0:0
-T:0:0 XO:0:0:S WS:0:0
-T:0:1 XO:0:1:S WS:1:0 XQ:0:0 WS:2:0 WS:0:1 XQ:0:1
-T:0:3 XO:0:3:S WW:1:0 XP:1:0:S
-S1:0:0:0
-T:0:2 XO:0:2:S WW:2:0
-S1:0:0:1
-WW:0:1 T:1:0 XO:1:0:S KG:0:V XQ:0:2 KQ:0
-T:1:1 XO:1:1:S XQ:0:3 VE:0 WW:1:1 WS:1:1 WS:2:1
-S1:0:0:2
-WW:2:1
-S1:0:0:3 XP:1:2:S ZO:0:0:S KG:1:V
-S1:0:1:0 S1:0:1:1 
-S1:0:1:2 KQ:1 XQ:1:0 XP:1:3:S
-T:1:2 T:1:3 XO:1:2:S XQ:1:1 XQ:1:2 XO:1:3:S
-S1:0:1:3 ZO:0:1:S
-XQ:1:3 S1:1:0:0 ZG:0:0
-S1:1:0:1 ZQ:0:0
-S1:1:0:2 S1:1:0:3 ZG:0:1 ZO:1:0:S
-S1:1:1:0 S1:1:1:1 ZQ:0:1 S1:1:1:2 S1:1:1:3 ZG:1:0 ZO:1:1:V
+LP:0:0:1 LS:0 LF:0 LF:1 LX:0:1 LX:0:3 LX:0:2 LP:0:1:3 LP:1:0:3 LX:1:0 LX:1:1 LK:0 LX:1:2 LV:0 LX:1:3 LK:1 LL:0
+W:8:0 WW:0:0
+T:0:0 XO:0:0:S W:2:1
+T:0:1 XO:0:1:S W:2:2 WA:0 XQ:0:0
+T:0:3 XO:0:3:S WA:1 XQ:0:1
+T:0:2
+S1:0:0:0 WW:1:0 WW:2:0 XO:0:2:S
+T:1:0 XO:1:0:S XQ:0:2 WW:0:1
+S1:0:0:1 XQ:0:3
+T:1:1 XO:1:1:S
+S1:0:0:2 KG:0:V VE:0 XP:1:2:S KQ:0
+S1:0:1:0
+S1:0:0:3 WW:1:1 XP:1:3:S WW:2:1
+S1:0:1:1 S1:0:1:2 ZO:0:0:S KG:1:V
+T:1:2 T:1:3 KQ:1
+S1:0:1:3 XO:1:2:S XO:1:3:S XQ:1:0 XQ:1:1 XQ:1:2 ZO:0:1:S XQ:1:3 ZG:0:0
+S1:1:0:0 S1:1:0:1 ZG:0:1 ZQ:0:0
+S1:1:0:2 S1:1:0:3 ZO:1:0:S ZQ:0:1
+S1:1:1:0 S1:1:1:1 S1:1:1:2 S1:1:1:3 ZG:1:0 ZO:1:1:V
 S2:0:0 ZQ:1:0
 S2:0:1 ME:0 ZG:1:1
 S2:0:2 ME:1 ZQ:1:1
-S2:0:3 ME:2
-S2:1:0 ME:3 S2:1:1 ME:4 S2:1:2 ME:5 S2:1:3 ME:6 ME:7
+S2:0:3 ME:2 S2:1:0 ME:3 S2:1:1 ME:4 S2:1:2 ME:5 S2:1:3 ME:6 ME:7
 """
 FLOPS = 2 * M * R * (J + K) + 2 * M * R * V
 
@@ -88,7 +84,6 @@ def tile_hotelling_contribution_monitor_s3_kernel(
         nc.vector.memset(ps_raw[:].bitcast(I32), 0)
         nc.vector.memset(dummy[:], 0.0)
         nc.vector.memset(warm[:], 0.0)
-        nc.scalar.activation(out=warm[:, 1:2], in_=warm[:, 0:1], func=ACT.Square)
         make_identity(nc, ident[:])
         nc.gpsimd.memset(ls[:].bitcast(I32), 0)
 
@@ -129,6 +124,7 @@ def tile_hotelling_contribution_monitor_s3_kernel(
 
         def load_plant_scales(unused):
             load_scales(ps_i, plant_scales, nc.scalar)
+            nc.scalar.activation(out=warm[:, 1:2], in_=warm[:, 0:1], func=ACT.Square)
 
         def load_load(unused):
             load_scales(ls_i, load_scales_hbm, nc.sync)
@@ -188,11 +184,21 @@ def tile_hotelling_contribution_monitor_s3_kernel(
                 in_=pw_raw[:, s, g, :].rearrange("p (m t b) -> p t m b", t=4, b=2),
             )
 
-        def scales_perm(g, s):
-            p_sc[g, s] = keep.tile([P, 512], U8, name="p_sc_%d_%d" % (g, s), align_bytes=64)
+        def scale_perm(g, s):
+            if s not in p_sc:
+                p_sc[s] = keep.tile([P, 3, 512], U8, name="p_sc_%d" % s, align_bytes=64)
             nc.vector.tensor_copy(
-                out=p_sc[g, s][:].rearrange("p (t m) -> p t m", t=4),
+                out=p_sc[s][:, g].rearrange("p (t m) -> p t m", t=4),
                 in_=ps_raw[:, R * g + 512 * s : R * g + 512 * s + 512].rearrange("p (m t) -> p t m", t=4),
+            )
+
+        def scales_perm(s):
+            p_sc[s] = keep.tile([P, 3, 512], U8, name="p_sc_%d" % s, align_bytes=64)
+            nc.vector.tensor_copy(
+                out=p_sc[s][:].rearrange("p g (t m) -> p t g m", t=4),
+                in_=ps_raw[:].rearrange("p (g c) -> p g c", g=3)[:, :, 512 * s : 512 * s + 512].rearrange(
+                    "p g (m t) -> p t g m", t=4
+                ),
             )
 
         def key_group(s, engine):
@@ -223,7 +229,7 @@ def tile_hotelling_contribution_monitor_s3_kernel(
                     lhs, lhs_sc = k_codes[s][:, cols].bitcast(FP8X4), k_sc[s][:, cols]
                 else:
                     lhs = p_codes[g, s][:, 256 * t : 256 * t + 256].bitcast(FP4X4)
-                    lhs_sc = p_sc[g, s][:, cols]
+                    lhs_sc = p_sc[s][:, g, cols]
                 nc.tensor.matmul_mx(
                     out=banks["s", h, s, t][:], lhsT=lhs, lhsT_scale=lhs_sc,
                     rhs=x_codes[h, g][:].bitcast(FP8X4), rhs_scale=x_sc[h, g][:], start=first, stop=last,
@@ -298,7 +304,7 @@ def tile_hotelling_contribution_monitor_s3_kernel(
             n = 5 if j == 7 else 4
             nc.scalar.activation(out=junk[:, 0:n], in_=acc[:, j, 0:n], func=ACT.Copy, scale=1.0 / V, accum_out=stat[:, j : j + 1])
 
-        def warm_up(n):
+        def warm_up(n, tag=0):
             bank = psum.tile([P, 512], F32, name="bank")
             for i in range(n):
                 nc.tensor.matmul(bank[:], lhsT=dummy[:, 0:128], rhs=dummy[:], start=True, stop=True)
@@ -309,7 +315,7 @@ def tile_hotelling_contribution_monitor_s3_kernel(
             nc.vector.tensor_tensor(out=zbias[:], in0=vecf[:, 0, :], in1=vecf[:, 1, :], op=ALU.mult)
 
         calls = {
-            "T": transposes, "XO": x_out, "XQ": x_quant, "WW": words_perm, "WS": scales_perm, "KG": key_group,
+            "T": transposes, "XO": x_out, "XQ": x_quant, "WW": words_perm, "WS": scale_perm, "WA": scales_perm, "KG": key_group,
             "KQ": key_quant, "S1": stage1, "ZO": z_out, "ZG": z_group, "ZQ": z_quant, "S2": stage2, "ME": mean, "VE": vectors, "W": warm_up, "LX": load_x, "LF": load_first, "LP": load_words_plant, "LK": load_key, "LV": load_vectors,
             "LS": load_plant_scales, "LL": load_load, "XP": x_order,
         }

from contextlib import ExitStack

import concourse.mybir as mybir
from concourse.masks import make_identity

F32 = mybir.dt.float32
BF16 = mybir.dt.bfloat16
I32 = mybir.dt.int32
U32 = mybir.dt.uint32
U8 = mybir.dt.uint8
FP8X4 = mybir.dt.float8_e4m3fn_x4
FP4X4 = mybir.dt.float4_e2m1fn_x4
ACT = mybir.ActivationFunctionType
ALU = mybir.AluOpType

P = 128
M, J, K, R, V = 1024, 512, 1536, 1024, 2048
KEY = 3
FIRST_G, LAST_G = 0, 3
VSQ = {(2, 1), (3, 1), (4, 1), (5, 1), (6, 1), (7, 1)}
ORDER = """
LP:0:0:1 LS:0 LF:0 LF:1 LX:0:1 LX:0:3 LX:0:2 LP:0:1:3 LP:1:0:3 LX:1:0 LX:1:1 LK:0 LX:1:2 LV:0 LX:1:3 LK:1 LL:0
W:8:0 WW:0:0
T:0:0 XO:0:0:S W:2:1
T:0:1 XO:0:1:S W:2:2 WA:0 XQ:0:0
T:0:3 XO:0:3:S WA:1 XQ:0:1
T:0:2
S1:0:0:0 WW:1:0 WW:2:0 XO:0:2:S
T:1:0 XO:1:0:S XQ:0:2 WW:0:1
S1:0:0:1 XQ:0:3
T:1:1 XO:1:1:S
S1:0:0:2 KG:0:V VE:0 XP:1:2:S KQ:0
S1:0:1:0
S1:0:0:3 WW:1:1 XP:1:3:S WW:2:1
S1:0:1:1 S1:0:1:2 ZO:0:0:S KG:1:V
T:1:2 T:1:3 KQ:1
S1:0:1:3 XO:1:2:S XO:1:3:S XQ:1:0 XQ:1:1 XQ:1:2 ZO:0:1:S XQ:1:3 ZG:0:0
S1:1:0:0 S1:1:0:1 ZG:0:1 ZQ:0:0
S1:1:0:2 S1:1:0:3 ZO:1:0:S ZQ:0:1
S1:1:1:0 S1:1:1:1 S1:1:1:2 S1:1:1:3 ZG:1:0 ZO:1:1:V
S2:0:0 ZQ:1:0
S2:0:1 ME:0 ZG:1:1
S2:0:2 ME:1 ZQ:1:1
S2:0:3 ME:2 S2:1:0 ME:3 S2:1:1 ME:4 S2:1:2 ME:5 S2:1:3 ME:6 ME:7
"""
FLOPS = 2 * M * R * (J + K) + 2 * M * R * V


def tile_hotelling_contribution_monitor_s3_kernel(
    tc, x_key, x_plant, w_key, plant_words, plant_scales, offset, inv_std, load_words, load_scales_hbm, out_0, out_1
):
    nc = tc.nc
    with ExitStack() as ctx:
        keep = ctx.enter_context(tc.tile_pool(name="keep", bufs=1))
        work = ctx.enter_context(tc.tile_pool(name="work", bufs=4))
        outp = ctx.enter_context(tc.tile_pool(name="outp", bufs=6))
        psum = ctx.enter_context(tc.psum_pool(name="psum", bufs=8))
        ctx.enter_context(tc.manual_schedule())

        xk_hbm = x_key.rearrange("(p j) k -> p j k", j=8)
        xp_hbm = x_plant.rearrange("(p j) k -> p j k", j=8)
        out_hbm = out_0.rearrange("(p j) v -> p j v", j=8)

        ident = keep.tile([P, P], F32, name="ident")
        warm = keep.tile([P, 2], F32, name="warm")
        ps_raw = keep.tile([P, 3 * R], U8, name="ps_raw", align_bytes=64)
        ls = keep.tile([P, 2 * V], U8, name="ls", align_bytes=64)
        lw = keep.tile([P, 2, 2 * V], U8, name="lw", align_bytes=64)
        off_b = keep.tile([P, 8], BF16, name="off_b")
        inv_b = keep.tile([P, 8], BF16, name="inv_b")
        vecf = keep.tile([P, 2, 8], F32, name="vecf")
        zbias = keep.tile([P, 8], F32, name="zbias")
        acc = keep.tile([P, 8, 5], F32, name="acc")
        junk = keep.tile([P, 5], F32, name="junk")
        stat = keep.tile([P, 8], F32, name="stat")
        x_raw = {}
        for h in range(2):
            for g in range(4):
                x_raw[h, g] = keep.tile([P, 4, 512], BF16, name="x_raw_%d_%d" % (h, g), align_bytes=64)
        pw_raw = keep.tile([P, 2, 3, 1024], U8, name="pw_raw", align_bytes=64)
        wk_raw = [keep.tile([P, 4, 512], BF16, name="wk_raw_%d" % s, align_bytes=64) for s in range(2)]

        dummy = keep.tile([P, 512], BF16, name="dummy")
        nc.vector.memset(ps_raw[:].bitcast(I32), 0)
        nc.vector.memset(dummy[:], 0.0)
        nc.vector.memset(warm[:], 0.0)
        make_identity(nc, ident[:])
        nc.gpsimd.memset(ls[:].bitcast(I32), 0)

        def load_x(h, g):
            rows = slice(4 * h, 4 * h + 4)
            src = xk_hbm[:, rows, :] if g == KEY else xp_hbm[:, rows, 512 * g : 512 * g + 512]
            nc.sync.dma_start(out=x_raw[h, g][:], in_=src)

        wk_hbm = w_key.rearrange("(p j) c -> p j c", j=4)
        ps_i = ps_raw[:].bitcast(I32).rearrange("p (g n) -> p g n", g=3)
        ls_i = ls[:].bitcast(I32).rearrange("p (g n) -> p g n", g=2)

        def load_scales(dst, src, queue):
            for q in range(4):
                queue.dma_start(
                    out=dst[32 * q : 32 * q + 4],
                    in_=src[:, 4 * q : 4 * q + 4, :].bitcast(I32).rearrange("g r n -> r g n"),
                )

        def load_vector(dst, src):
            nc.sync.dma_start(
                out=dst[:].rearrange("p (s t) -> p s t", s=2), in_=src.rearrange("(s p t) -> p s t", s=2, t=4)
            )

        def load_words_plant(s, g0, g1):
            src = plant_words.rearrange("g p (s b) -> s p g b", s=2)
            nc.sync.dma_start(out=pw_raw[:, s, g0:g1, :], in_=src[s, :, g0:g1, :])

        def load_first(rr):
            nc.sync.dma_start(out=x_raw[0, 0][:, 2 * rr : 2 * rr + 2, :], in_=xp_hbm[:, 2 * rr : 2 * rr + 2, 0:512])

        def load_key(s):
            nc.sync.dma_start(out=wk_raw[s][:], in_=wk_hbm[:, :, 512 * s : 512 * s + 512])

        def load_vectors(unused):
            load_vector(off_b, offset)
            load_vector(inv_b, inv_std)

        def load_plant_scales(unused):
            load_scales(ps_i, plant_scales, nc.scalar)
            nc.scalar.activation(out=warm[:, 1:2], in_=warm[:, 0:1], func=ACT.Square)

        def load_load(unused):
            load_scales(ls_i, load_scales_hbm, nc.sync)
            for s in range(2):
                nc.sync.dma_start(out=lw[:, s, :], in_=load_words[s])

        banks = {}
        x_perm = {}
        x_grp, x_codes, x_sc = {}, {}, {}
        p_sc = {}
        p_codes, k_grp, k_codes, k_sc = {}, {}, {}, {}
        z_raw, z_grp, z_codes, z_sc = {}, {}, {}, {}

        def transposes(h, g):
            words = x_raw[h, g][:].bitcast(F32)
            for b in range(2):
                if (h, g) in x_perm:
                    perm = x_perm[h, g]
                bank = psum.tile([P, 512], F32, name="bank")
                banks["x", h, g, b] = bank
                for rr in range(2):
                    for u in range(2):
                        c = 256 * rr + 128 * u
                        if (h, g) in x_perm:
                            nc.tensor.transpose(bank[:, c : c + 128], perm[:, 2 * b + rr, u, :], ident[:])
                        else:
                            nc.tensor.transpose(bank[:, c : c + 128], words[:, 2 * b + rr, u::2], ident[:])

        def x_order(h, g, engine):
            x_perm[h, g] = work.tile([P, 4, 2, 128], F32, name="x_perm", align_bytes=64)
            src = x_raw[h, g][:].bitcast(F32).rearrange("p r (n u) -> p r u n", u=2)
            if engine == "S":
                nc.scalar.copy(out=x_perm[h, g][:], in_=src)
            else:
                nc.vector.tensor_copy(out=x_perm[h, g][:], in_=src)

        def x_out(h, g, engine):
            x_grp[h, g] = work.tile([P, 2048], BF16, name="x_grp", align_bytes=64)
            words = x_grp[h, g][:].bitcast(F32)
            for b in range(2):
                src = banks["x", h, g, b][:].rearrange("p (r u n) -> p r n u", r=2, u=2)
                dst = words[:, 512 * b : 512 * b + 512].rearrange("p (r n u) -> p r n u", r=2, u=2)
                if engine == "S" or (engine == "SV" and b == 0):
                    nc.scalar.copy(out=dst, in_=src)
                else:
                    nc.vector.tensor_copy(out=dst, in_=src)

        def x_quant(h, g):
            x_codes[h, g] = keep.tile([P, 512], U32, name="x_codes_%d_%d" % (h, g), align_bytes=64)
            x_sc[h, g] = keep.tile([P, 512], U8, name="x_sc_%d_%d" % (h, g), align_bytes=64)
            nc.vector.quantize_mx(out=x_codes[h, g][:].bitcast(FP8X4), scales=x_sc[h, g][:], in_=x_grp[h, g][:])

        def words_perm(g, s):
            p_codes[g, s] = keep.tile([P, 1024], U8, name="p_codes_%d_%d" % (g, s), align_bytes=64)
            nc.vector.tensor_copy(
                out=p_codes[g, s][:].rearrange("p (t m b) -> p t m b", t=4, b=2),
                in_=pw_raw[:, s, g, :].rearrange("p (m t b) -> p t m b", t=4, b=2),
            )

        def scale_perm(g, s):
            if s not in p_sc:
                p_sc[s] = keep.tile([P, 3, 512], U8, name="p_sc_%d" % s, align_bytes=64)
            nc.vector.tensor_copy(
                out=p_sc[s][:, g].rearrange("p (t m) -> p t m", t=4),
                in_=ps_raw[:, R * g + 512 * s : R * g + 512 * s + 512].rearrange("p (m t) -> p t m", t=4),
            )

        def scales_perm(s):
            p_sc[s] = keep.tile([P, 3, 512], U8, name="p_sc_%d" % s, align_bytes=64)
            nc.vector.tensor_copy(
                out=p_sc[s][:].rearrange("p g (t m) -> p t g m", t=4),
                in_=ps_raw[:].rearrange("p (g c) -> p g c", g=3)[:, :, 512 * s : 512 * s + 512].rearrange(
                    "p g (m t) -> p t g m", t=4
                ),
            )

        def key_group(s, engine):
            k_grp[s] = work.tile([P, 2048], BF16, name="k_grp", align_bytes=64)
            dst = k_grp[s][:].rearrange("p (t m j) -> p t m j", t=4, j=4)
            src = wk_raw[s][:].rearrange("p j (m t) -> p t m j", t=4)
            if engine == "S":
                nc.scalar.copy(out=dst, in_=src)
            elif engine == "V":
                nc.vector.tensor_copy(out=dst, in_=src)
            else:
                nc.scalar.copy(out=dst[:, 0:2], in_=src[:, 0:2])
                nc.vector.tensor_copy(out=dst[:, 2:4], in_=src[:, 2:4])

        def key_quant(s):
            k_codes[s] = keep.tile([P, 512], U32, name="k_codes_%d" % s, align_bytes=64)
            k_sc[s] = keep.tile([P, 512], U8, name="k_sc_%d" % s, align_bytes=64)
            nc.vector.quantize_mx(out=k_codes[s][:].bitcast(FP8X4), scales=k_sc[s][:], in_=k_grp[s][:])

        def stage1(h, s, g):
            first, last = g == FIRST_G, g == LAST_G
            for t in range(4):
                if first:
                    bank = psum.tile([P, 512], F32, name="bank")
                    banks["s", h, s, t] = bank
                cols = slice(128 * t, 128 * t + 128)
                if g == KEY:
                    lhs, lhs_sc = k_codes[s][:, cols].bitcast(FP8X4), k_sc[s][:, cols]
                else:
                    lhs = p_codes[g, s][:, 256 * t : 256 * t + 256].bitcast(FP4X4)
                    lhs_sc = p_sc[s][:, g, cols]
                nc.tensor.matmul_mx(
                    out=banks["s", h, s, t][:], lhsT=lhs, lhsT_scale=lhs_sc,
                    rhs=x_codes[h, g][:].bitcast(FP8X4), rhs_scale=x_sc[h, g][:], start=first, stop=last,
                )

        def z_out(h, s, engine):
            z_raw[h, s] = work.tile([P, 4, 512], BF16, name="z_raw", align_bytes=64)
            for t in range(4):
                c = 4 * s + t
                if engine == "S" or (engine == "SV" and t < 2):
                    nc.scalar.activation(
                        out=z_raw[h, s][:, t, :], in_=banks["s", h, s, t][:], func=ACT.Identity,
                        bias=zbias[:, c : c + 1], scale=vecf[:, 1, c : c + 1],
                    )
                else:
                    nc.vector.tensor_scalar(
                        out=z_raw[h, s][:, t, :], in0=banks["s", h, s, t][:], scalar1=vecf[:, 0, c : c + 1],
                        scalar2=vecf[:, 1, c : c + 1], op0=ALU.add, op1=ALU.mult,
                    )

        def z_group(h, s):
            z_grp[h, s] = work.tile([P, 2048], BF16, name="z_grp", align_bytes=64)
            nc.vector.tensor_copy(
                out=z_grp[h, s][:].rearrange("p (n t) -> p n t", t=4), in_=z_raw[h, s][:].rearrange("p t n -> p n t")
            )

        def z_quant(h, s):
            z_codes[h, s] = keep.tile([P, 512], U32, name="z_codes_%d_%d" % (h, s), align_bytes=64)
            z_sc[h, s] = keep.tile([P, 512], U8, name="z_sc_%d_%d" % (h, s), align_bytes=64)
            nc.vector.quantize_mx(out=z_codes[h, s][:].bitcast(FP8X4), scales=z_sc[h, s][:], in_=z_grp[h, s][:])

        def stage2(h, r):
            j = 4 * h + r
            cols = slice(128 * r, 128 * r + 128)
            for w in range(2):
                res = outp.tile([P, 1024], F32, name="res")
                for vv in range(2):
                    v = 2 * w + vv
                    bank = psum.tile([P, 512], F32, name="bank")
                    for s in range(2):
                        nc.tensor.matmul_mx(
                            out=bank[:], lhsT=z_codes[h, s][:, cols].bitcast(FP8X4), lhsT_scale=z_sc[h, s][:, cols],
                            rhs=lw[:, s, 1024 * v : 1024 * v + 1024].bitcast(FP4X4),
                            rhs_scale=ls[:, V * s + 512 * v : V * s + 512 * v + 512], start=s == 0, stop=s == 1,
                        )
                    half = res[:, 512 * vv : 512 * vv + 512]
                    if (j, v) == (7, 3):
                        for c in (0, 256):
                            nc.scalar.activation(
                                out=half[:, c : c + 256], in_=bank[:, c : c + 256], func=ACT.Square,
                                accum_out=acc[:, j, 3 + c // 256 : 4 + c // 256],
                            )
                            nc.sync.dma_start(
                                out=out_hbm[:, j, 512 * v + c : 512 * v + c + 256], in_=half[:, c : c + 256]
                            )
                        continue
                    if (j, v) in VSQ:
                        copy = work.tile([P, 512], F32, name="copy")
                        nc.vector.tensor_copy(out=copy[:], in_=bank[:])
                        nc.vector.scalar_tensor_tensor(
                            out=half, in0=bank[:], scalar=1.0, in1=copy[:], op0=ALU.mult, op1=ALU.mult,
                            accum_out=acc[:, j, v : v + 1],
                        )
                    else:
                        nc.scalar.activation(out=half, in_=bank[:], func=ACT.Square, accum_out=acc[:, j, v : v + 1])
                    if j == 7:
                        nc.sync.dma_start(out=out_hbm[:, j, 512 * v : 512 * v + 512], in_=half)
                if j != 7:
                    nc.sync.dma_start(out=out_hbm[:, j, 1024 * w : 1024 * w + 1024], in_=res[:])

        def mean(j):
            n = 5 if j == 7 else 4
            nc.scalar.activation(out=junk[:, 0:n], in_=acc[:, j, 0:n], func=ACT.Copy, scale=1.0 / V, accum_out=stat[:, j : j + 1])

        def warm_up(n, tag=0):
            bank = psum.tile([P, 512], F32, name="bank")
            for i in range(n):
                nc.tensor.matmul(bank[:], lhsT=dummy[:, 0:128], rhs=dummy[:], start=True, stop=True)

        def vectors(unused):
            nc.vector.tensor_copy(out=vecf[:, 0, :], in_=off_b[:])
            nc.vector.tensor_copy(out=vecf[:, 1, :], in_=inv_b[:])
            nc.vector.tensor_tensor(out=zbias[:], in0=vecf[:, 0, :], in1=vecf[:, 1, :], op=ALU.mult)

        calls = {
            "T": transposes, "XO": x_out, "XQ": x_quant, "WW": words_perm, "WS": scale_perm, "WA": scales_perm, "KG": key_group,
            "KQ": key_quant, "S1": stage1, "ZO": z_out, "ZG": z_group, "ZQ": z_quant, "S2": stage2, "ME": mean, "VE": vectors, "W": warm_up, "LX": load_x, "LF": load_first, "LP": load_words_plant, "LK": load_key, "LV": load_vectors,
            "LS": load_plant_scales, "LL": load_load, "XP": x_order,
        }
        for step in ORDER.split():
            parts = step.split(":")
            args = [a if a in ("S", "V", "SV") else int(a) for a in parts[1:]]
            calls[parts[0]](*args)
        nc.sync.dma_start(out=out_1.rearrange("(p j) -> p j", j=8), in_=stat[:])
